import numpy as np
import ml_dtypes


def mxq(x, axis, fmt="e4m3"):
    dtype, down = {"e4m3": (ml_dtypes.float8_e4m3fn, 7), "e5m2": (ml_dtypes.float8_e5m2, 14)}[fmt]
    v = np.moveaxis(np.asarray(x, np.float32).astype(ml_dtypes.bfloat16).astype(np.float64), axis, -1)
    blocks = v.reshape(v.shape[:-1] + (-1, 32))
    amax = np.abs(blocks).max(-1, keepdims=True)
    byte = np.maximum(np.where(amax > 0, np.frexp(amax)[1] - 1 + 127, 0) - down, 1)
    scale = np.exp2(byte - 127.0)
    codes = (blocks / scale).astype(np.float32).astype(dtype).astype(np.float64)
    return np.moveaxis((codes * scale).reshape(v.shape), -1, axis)


WIDE = False


def mx_kscale(k):
    if not WIDE:
        return np.ones(k)
    levels = np.array([30, -30])
    if k % 512:
        return np.exp2(np.random.permutation(np.resize(levels, k // 32))).repeat(32)
    a = np.empty((k // 512, 16))
    for p in range(k // 512):
        a[p, :8] = np.random.permutation(np.resize(levels, 8))
        for g in range(8):
            far = levels[np.abs(levels - a[p, g]) >= 10]
            a[p, g + 8] = far[np.random.randint(len(far))]
    return np.exp2(a.ravel()).repeat(32)


def f64(x):
    return np.asarray(x).astype(np.float64)


def striped(idx):
    return np.tile(np.asarray(idx).reshape(-1, 16).T, (8, 1)).astype(np.uint16)


def unstriped(offs):
    return offs[:16].T.reshape(-1).astype(np.int64)


E2M1 = np.array([0.0, 0.5, 1.0, 1.5, 2.0, 3.0, 4.0, 6.0, -0.0, -0.5, -1.0, -1.5, -2.0, -3.0, -4.0, -6.0])


def pack_weight(w, fmt):
    k, n = w.shape
    w = f64(np.asarray(w, np.float32).astype(ml_dtypes.bfloat16)).reshape(k // 32, 32, n)
    amax = np.abs(w).max(1)
    if fmt == "e4m3":
        byte = np.frexp(amax)[1] - 1 + 127 - 7
    else:
        mant, ex = np.frexp(amax / 6.0)
        byte = np.where(mant > 0.5, ex, ex - 1) + 127
    byte = np.clip(np.where(amax > 0, byte, 1), 1, 254)
    scaled = (w * np.exp2(127.0 - byte)[:, None, :]).reshape(k, n).astype(np.float32)
    by_word = np.ascontiguousarray(scaled.reshape(k // 512, 128, 4, n).transpose(0, 1, 3, 2))
    if fmt == "e4m3":
        words = by_word.astype(ml_dtypes.float8_e4m3fn).view(np.uint8)
    else:
        c = by_word.astype(ml_dtypes.float4_e2m1fn).view(np.uint8) & 0xF
        words = (c[..., 0::2] | (c[..., 1::2] << 4)).reshape(k // 512, 128, 2 * n)
    return np.ascontiguousarray(words), np.ascontiguousarray(byte.astype(np.uint8).reshape(k // 512, 16, n))


def unpack_weight(words, scales, fmt):
    g, _, n = scales.shape
    words = np.ascontiguousarray(words).reshape(g, 128, n, -1)
    if fmt == "e4m3":
        vals = words.view(ml_dtypes.float8_e4m3fn).astype(np.float64)
    else:
        nib = np.empty((g, 128, n, 4), np.uint8)
        nib[..., 0::2] = words & 0xF
        nib[..., 1::2] = words >> 4
        vals = E2M1[nib]
    vals = vals * np.repeat(np.exp2(scales.astype(np.float64) - 127.0), 8, axis=1)[..., None]
    return vals.transpose(0, 1, 3, 2).reshape(g * 512, n)


N, R, K, J, I = 1024, 512, 512, 1024, 512


def setup_inputs():
    n = np.random.standard_normal
    idx = np.random.permutation(J)[:I]
    fn = mx_kscale(N)
    fr = mx_kscale(R)
    gp = pack_weight(n((N, I)) / fn[:, None], "e4m3")
    wdp = pack_weight(n((N, R)) * 1 / np.sqrt(N) * fn[:, None], "e2m1")
    wup = pack_weight(n((R, K)) * 1 / np.sqrt(R) / fr[:, None], "e4m3")
    return {
        "g_words": gp[0],
        "g_scales": gp[1],
        "wd_words": wdp[0],
        "wd_scales": wdp[1],
        "z": (n((R, J)) * fr[:, None]).astype(np.float32),
        "wu_words": wup[0],
        "wu_scales": wup[1],
        "run": (0.5 * n((K, J))).astype(np.float32),
        "offs": striped(idx),
    }


def reference(g_words, g_scales, wd_words, wd_scales, z, wu_words, wu_scales, run, offs):
    idx = unstriped(offs)
    gu = unpack_weight(g_words, g_scales, "e4m3")
    wdu = unpack_weight(wd_words, wd_scales, "e2m1")
    wuu = unpack_weight(wu_words, wu_scales, "e4m3")
    d = wdu.T @ gu
    dp = np.zeros((R, J))
    dp[:, idx] = d
    dz = 2.0 * dp * np.maximum(f64(z), 0.0)
    dzq = mxq(dz, 0, "e5m2")
    p = wuu.T @ dzq
    y = p + f64(run)
    return y

@@ -1,0 +1,157 @@
+from contextlib import ExitStack
+
+import concourse.mybir as mybir
+
+N, R, K, J, I = 1024, 512, 512, 1024, 512
+FLOPS = 2 * N * R * I + 2 * R * K * J
+
+F32 = mybir.dt.float32
+BF16 = mybir.dt.bfloat16
+I32 = mybir.dt.int32
+U16 = mybir.dt.uint16
+U8 = mybir.dt.uint8
+E4M3 = mybir.dt.float8_e4m3fn_x4
+E5M2 = mybir.dt.float8_e5m2_x4
+E2M1 = mybir.dt.float4_e2m1fn_x4
+MULT = mybir.AluOpType.mult
+ADD = mybir.AluOpType.add
+RELU = mybir.ActivationFunctionType.Relu
+
+P = 128
+PACK = 4
+PASSES = N // (P * PACK)
+BANK = 512
+QUARTER = 256
+FIRST_CUTS = ((0, 128), (128, 256), (256, 512))
+
+
+def load_scale_rows(queues, plane, scales):
+    for quad, queue in enumerate(queues):
+        queue.dma_start(
+            out=plane[32 * quad : 32 * quad + 4].bitcast(I32),
+            in_=scales[:, 4 * quad : 4 * quad + 4, :].rearrange("z r c -> r z c").bitcast(I32),
+        )
+
+
+def tile_list_listed_slots_back_through_rest_kernel(
+    tc, g_words, g_scales, wd_words, wd_scales, z, wu_words, wu_scales, run, offs, out
+):
+    nc = tc.nc
+    with ExitStack() as ctx:
+        keep = ctx.enter_context(tc.tile_pool(name="keep", bufs=1))
+        psum = ctx.enter_context(tc.psum_pool(name="psum", bufs=8))
+
+        offsets = keep.tile([P, I // 16], U16, name="offsets")
+        nc.sync.dma_start(offsets[:], offs)
+
+        wd_raw = keep.tile([P, PASSES, 2 * R], U8, name="wd_raw", tag="then_z", align_bytes=64)
+        wd_plane_raw = keep.tile([P, PASSES, R], U8, name="wd_plane_raw", tag="then_run", align_bytes=64)
+        g_codes = keep.tile([P, PASSES, I], I32, name="g_codes", tag="then_wu", align_bytes=64)
+        g_plane = keep.tile([P, PASSES, I], U8, name="g_plane", tag="then_wu_plane", align_bytes=64)
+
+        nc.vector.memset(wd_plane_raw[:].bitcast(I32), 0)
+        nc.gpsimd.memset(g_plane[:].bitcast(I32), 0)
+        nc.sync.dma_start(out=wd_raw[:].bitcast(I32), in_=wd_words.rearrange("z p c -> p z c").bitcast(I32))
+        nc.sync.dma_start(out=g_codes[:], in_=g_words.rearrange("z p c t -> p z (c t)").bitcast(I32))
+        load_scale_rows((nc.scalar,) * 4, wd_plane_raw, wd_scales)
+        load_scale_rows((nc.sync, nc.sync, nc.gpsimd, nc.gpsimd), g_plane, g_scales)
+
+        pages = [keep.tile([P, J], F32, name=f"page{t}") for t in range(PACK)]
+        for t in range(PACK):
+            nc.vector.memset(pages[t][:], 0.0)
+
+        wd_codes = [keep.tile([P, PASSES, 2 * P], U8, name=f"wd_codes{t}", align_bytes=64) for t in range(PACK)]
+        wd_planes = [keep.tile([P, PASSES, P], U8, name=f"wd_plane{t}", align_bytes=64) for t in range(PACK)]
+        wd_dealt = wd_raw[:].bitcast(U16).rearrange("p z (m t) -> p t z m", t=PACK)
+        plane_dealt = wd_plane_raw[:].rearrange("p z (m t) -> p t z m", t=PACK)
+        for t in range(PACK):
+            nc.vector.tensor_copy(out=wd_codes[t][:].bitcast(U16), in_=wd_dealt[:, t])
+            nc.vector.tensor_copy(out=wd_planes[t][:], in_=plane_dealt[:, t])
+
+        z_rows = keep.tile([P, PACK, J], F32, name="z_rows", tag="then_z", align_bytes=64)
+        z_dealt = z.rearrange("(p t) j -> p t j", t=PACK)
+        for t in range(PACK):
+            nc.sync.dma_start(out=z_rows[:, t, :], in_=z_dealt[:, t, :])
+        run_rows = keep.tile([P, K // P, J], F32, name="run_rows", tag="then_run", align_bytes=64)
+        for m in range(K // P):
+            nc.sync.dma_start(out=run_rows[:, m, :], in_=run[m * P : (m + 1) * P, :])
+
+        def first_product(t, lo, hi):
+            acc = psum.tile([P, BANK], F32, name="acc")
+            step = BANK if hi - lo == BANK else P
+            for c in range(lo, hi, step):
+                for a in range(PASSES):
+                    nc.tensor.matmul_mx(
+                        out=acc[:, c - lo : c - lo + step],
+                        lhsT=wd_codes[t][:, a, :].bitcast(E2M1),
+                        lhsT_scale=wd_planes[t][:, a, :],
+                        rhs=g_codes[:, a, c : c + step].bitcast(E4M3),
+                        rhs_scale=g_plane[:, a, c : c + step],
+                        start=(a == 0),
+                        stop=(a == PASSES - 1),
+                    )
+            d = keep.tile([P, hi - lo], F32, name=f"d{t}_{lo}")
+            nc.scalar.copy(out=d[:], in_=acc[:, : hi - lo])
+            nc.vector.tensor_copy(pages[t][:].indirect(offsets[:, lo // 16 : hi // 16]), d[:])
+
+        quarters = J // QUARTER
+        slopes = [keep.tile([P, J], F32, name=f"slope{t}") for t in range(PACK)]
+        low_planes = keep.tile([P, 2, J], BF16, name="low_planes")
+        pairs = [keep.tile([P, 2, QUARTER, 2], BF16, name=f"pairs{q}") for q in range(quarters)]
+
+        for t in range(PACK):
+            for lo, hi in FIRST_CUTS if t == 0 else ((0, I),):
+                first_product(t, lo, hi)
+            nc.scalar.activation(out=slopes[t][:], in_=z_rows[:, t, :], func=RELU, scale=2.0)
+            if t < 2:
+                nc.vector.tensor_tensor(out=low_planes[:, t, :], in0=pages[t][:], in1=slopes[t][:], op=MULT)
+            if t == 1:
+                for q in range(quarters):
+                    cols = slice(q * QUARTER, (q + 1) * QUARTER)
+                    nc.scalar.copy(out=pairs[q][:, 0], in_=low_planes[:, :, cols].rearrange("p e j -> p j e"))
+            if t == 2:
+                for q in range(quarters):
+                    cols = slice(q * QUARTER, (q + 1) * QUARTER)
+                    nc.vector.tensor_tensor(out=pairs[q][:, 1, :, 0], in0=pages[t][:, cols], in1=slopes[t][:, cols], op=MULT)
+
+        wu_codes = keep.tile([P, K], I32, name="wu_codes", tag="then_wu", align_bytes=64)
+        wu_plane = keep.tile([P, 1, K], U8, name="wu_plane", tag="then_wu_plane", align_bytes=64)
+        nc.sync.dma_start(out=wu_codes[:], in_=wu_words[0].rearrange("p c t -> p (c t)").bitcast(I32))
+        nc.gpsimd.memset(wu_plane[:].bitcast(I32), 0)
+        load_scale_rows((nc.sync,) * 4, wu_plane, wu_scales)
+
+        dz_codes = [keep.tile([P, BANK], I32, name=f"dz_codes{h}", align_bytes=64) for h in range(J // BANK)]
+        dz_planes = [keep.tile([P, BANK], U8, name=f"dz_plane{h}", align_bytes=64) for h in range(J // BANK)]
+        sums = []
+        for q in range(quarters):
+            cols = slice(q * QUARTER, (q + 1) * QUARTER)
+            h, part = divmod(q * QUARTER, BANK)
+            nc.vector.tensor_tensor(out=pairs[q][:, 1, :, 1], in0=pages[3][:, cols], in1=slopes[3][:, cols], op=MULT)
+            grouped = keep.tile([P, QUARTER * PACK], BF16, name=f"grouped{q}", align_bytes=64)
+            nc.scalar.copy(
+                out=grouped[:].bitcast(F32).rearrange("p (j u) -> p j u", u=2),
+                in_=pairs[q][:].rearrange("p u j e -> p u (j e)").bitcast(F32).rearrange("p u j -> p j u"),
+            )
+            nc.vector.quantize_mx(
+                out=dz_codes[h][:, part : part + QUARTER].bitcast(E5M2),
+                scales=dz_planes[h][:, part : part + QUARTER],
+                in_=grouped[:],
+            )
+            if part + QUARTER == BANK:
+                for m in range(K // P):
+                    acc = psum.tile([P, BANK], F32, name="acc")
+                    nc.tensor.matmul_mx(
+                        out=acc[:],
+                        lhsT=wu_codes[:, m * P : (m + 1) * P].bitcast(E4M3),
+                        lhsT_scale=wu_plane[:, 0, m * P : (m + 1) * P],
+                        rhs=dz_codes[h][:].bitcast(E5M2),
+                        rhs_scale=dz_planes[h][:],
+                        start=True,
+                        stop=True,
+                    )
+                    sums.append((h, m, acc))
+        for h, m, acc in sums:
+            cols = slice(h * BANK, (h + 1) * BANK)
+            result = keep.tile([P, BANK], F32, name=f"result{h}_{m}")
+            nc.vector.tensor_tensor(out=result[:], in0=acc[:], in1=run_rows[:, m, cols], op=ADD)
+            nc.sync.dma_start(out=out[m * P : (m + 1) * P, cols], in_=result[:])

@@ -43,21 +43,19 @@ def tile_list_listed_slots_back_through_rest_kernel(
 
         offsets = keep.tile([P, I // 16], U16, name="offsets")
         nc.sync.dma_start(offsets[:], offs)
-
         wd_raw = keep.tile([P, PASSES, 2 * R], U8, name="wd_raw", tag="then_z", align_bytes=64)
         wd_plane_raw = keep.tile([P, PASSES, R], U8, name="wd_plane_raw", tag="then_run", align_bytes=64)
         g_codes = keep.tile([P, PASSES, I], I32, name="g_codes", tag="then_wu", align_bytes=64)
         g_plane = keep.tile([P, PASSES, I], U8, name="g_plane", tag="then_wu_plane", align_bytes=64)
 
-        nc.vector.memset(wd_plane_raw[:].bitcast(I32), 0)
-        nc.gpsimd.memset(g_plane[:].bitcast(I32), 0)
+        nc.gpsimd.memset(wd_plane_raw[:].bitcast(I32), 0)
+        load_scale_rows((nc.sync, nc.scalar, nc.scalar, nc.scalar), g_plane, g_scales)
         nc.sync.dma_start(out=wd_raw[:].bitcast(I32), in_=wd_words.rearrange("z p c -> p z c").bitcast(I32))
         nc.sync.dma_start(out=g_codes[:], in_=g_words.rearrange("z p c t -> p z (c t)").bitcast(I32))
-        load_scale_rows((nc.scalar,) * 4, wd_plane_raw, wd_scales)
-        load_scale_rows((nc.sync, nc.sync, nc.gpsimd, nc.gpsimd), g_plane, g_scales)
+        load_scale_rows((nc.sync,) * 4, wd_plane_raw, wd_scales)
 
-        pages = [keep.tile([P, J], F32, name=f"page{t}") for t in range(PACK)]
-        for t in range(PACK):
+        pages = [keep.tile([P, J], F32, name=f"page{t}") for t in range(2)]
+        for t in range(2):
             nc.vector.memset(pages[t][:], 0.0)
 
         wd_codes = [keep.tile([P, PASSES, 2 * P], U8, name=f"wd_codes{t}", align_bytes=64) for t in range(PACK)]
@@ -90,21 +88,26 @@ def tile_list_listed_slots_back_through_rest_kernel(
                         start=(a == 0),
                         stop=(a == PASSES - 1),
                     )
-            d = keep.tile([P, hi - lo], F32, name=f"d{t}_{lo}")
+            d = keep.tile([P, hi - lo], F32, name=f"d{t}_{lo}", tag=f"d{t}_{lo}")
             nc.scalar.copy(out=d[:], in_=acc[:, : hi - lo])
             nc.vector.tensor_copy(pages[t][:].indirect(offsets[:, lo // 16 : hi // 16]), d[:])
 
         quarters = J // QUARTER
         slopes = [keep.tile([P, J], F32, name=f"slope{t}") for t in range(PACK)]
         low_planes = keep.tile([P, 2, J], BF16, name="low_planes")
+        third = [keep.tile([P, QUARTER], BF16, name=f"third{q}") for q in range(quarters)]
         pairs = [keep.tile([P, 2, QUARTER, 2], BF16, name=f"pairs{q}") for q in range(quarters)]
 
         for t in range(PACK):
             for lo, hi in FIRST_CUTS if t == 0 else ((0, I),):
                 first_product(t, lo, hi)
+            if t == 0:
+                for later, lo in ((2, 0), (3, 128)):
+                    pages.append(keep.tile([P, J], F32, name=f"page{later}", tag=f"d0_{lo}"))
+                    nc.gpsimd.memset(pages[later][:], 0.0)
             nc.scalar.activation(out=slopes[t][:], in_=z_rows[:, t, :], func=RELU, scale=2.0)
             if t < 2:
-                nc.vector.tensor_tensor(out=low_planes[:, t, :], in0=pages[t][:], in1=slopes[t][:], op=MULT)
+                nc.gpsimd.tensor_tensor(out=low_planes[:, t, :], in0=pages[t][:], in1=slopes[t][:], op=MULT)
             if t == 1:
                 for q in range(quarters):
                     cols = slice(q * QUARTER, (q + 1) * QUARTER)
@@ -112,12 +115,12 @@ def tile_list_listed_slots_back_through_rest_kernel(
             if t == 2:
                 for q in range(quarters):
                     cols = slice(q * QUARTER, (q + 1) * QUARTER)
-                    nc.vector.tensor_tensor(out=pairs[q][:, 1, :, 0], in0=pages[t][:, cols], in1=slopes[t][:, cols], op=MULT)
+                    nc.gpsimd.tensor_tensor(out=third[q][:], in0=pages[t][:, cols], in1=slopes[t][:, cols], op=MULT)
+                    nc.scalar.copy(out=pairs[q][:, 1], in_=third[q][:].unsqueeze(2).to_broadcast([P, QUARTER, 2]))
 
         wu_codes = keep.tile([P, K], I32, name="wu_codes", tag="then_wu", align_bytes=64)
         wu_plane = keep.tile([P, 1, K], U8, name="wu_plane", tag="then_wu_plane", align_bytes=64)
         nc.sync.dma_start(out=wu_codes[:], in_=wu_words[0].rearrange("p c t -> p (c t)").bitcast(I32))
-        nc.gpsimd.memset(wu_plane[:].bitcast(I32), 0)
         load_scale_rows((nc.sync,) * 4, wu_plane, wu_scales)
 
         dz_codes = [keep.tile([P, BANK], I32, name=f"dz_codes{h}", align_bytes=64) for h in range(J // BANK)]

@@ -22,7 +22,7 @@ PACK = 4
 PASSES = N // (P * PACK)
 BANK = 512
 QUARTER = 256
-FIRST_CUTS = ((0, 128), (128, 256), (256, 512))
+EARLY = 128
 
 
 def load_scale_rows(queues, plane, scales):
@@ -49,10 +49,12 @@ def tile_list_listed_slots_back_through_rest_kernel(
         g_plane = keep.tile([P, PASSES, I], U8, name="g_plane", tag="then_wu_plane", align_bytes=64)
 
         nc.gpsimd.memset(wd_plane_raw[:].bitcast(I32), 0)
-        load_scale_rows((nc.sync, nc.scalar, nc.scalar, nc.scalar), g_plane, g_scales)
+        load_scale_rows((nc.sync, nc.sync, nc.scalar, nc.scalar), g_plane, g_scales)
         nc.sync.dma_start(out=wd_raw[:].bitcast(I32), in_=wd_words.rearrange("z p c -> p z c").bitcast(I32))
-        nc.sync.dma_start(out=g_codes[:], in_=g_words.rearrange("z p c t -> p z (c t)").bitcast(I32))
+        g_rows = g_words.rearrange("z p c t -> p z (c t)").bitcast(I32)
+        nc.sync.dma_start(out=g_codes[:, :, :EARLY], in_=g_rows[:, :, :EARLY])
         load_scale_rows((nc.sync,) * 4, wd_plane_raw, wd_scales)
+        nc.sync.dma_start(out=g_codes[:, :, EARLY:], in_=g_rows[:, :, EARLY:])
 
         pages = [keep.tile([P, J], F32, name=f"page{t}") for t in range(2)]
         for t in range(2):
@@ -88,35 +90,39 @@ def tile_list_listed_slots_back_through_rest_kernel(
                         start=(a == 0),
                         stop=(a == PASSES - 1),
                     )
-            d = keep.tile([P, hi - lo], F32, name=f"d{t}_{lo}", tag=f"d{t}_{lo}")
+            d = keep.tile([P, hi - lo], F32, name=f"d{t}_{lo}", tag=f"d{t}_{lo}" if hi == EARLY else f"rest{t}")
             nc.scalar.copy(out=d[:], in_=acc[:, : hi - lo])
             nc.vector.tensor_copy(pages[t][:].indirect(offsets[:, lo // 16 : hi // 16]), d[:])
 
         quarters = J // QUARTER
         slopes = [keep.tile([P, J], F32, name=f"slope{t}") for t in range(PACK)]
-        low_planes = keep.tile([P, 2, J], BF16, name="low_planes")
-        third = [keep.tile([P, QUARTER], BF16, name=f"third{q}") for q in range(quarters)]
+        low_planes = [keep.tile([P, 2, BANK], BF16, name=f"low_planes{h}") for h in range(J // BANK)]
         pairs = [keep.tile([P, 2, QUARTER, 2], BF16, name=f"pairs{q}") for q in range(quarters)]
 
+        for t in range(2):
+            first_product(t, 0, EARLY)
+            pages.append(keep.tile([P, J], F32, name=f"page{t + 2}", tag=f"d{t}_0"))
+            nc.gpsimd.memset(pages[t + 2][:], 0.0)
         for t in range(PACK):
-            for lo, hi in FIRST_CUTS if t == 0 else ((0, I),):
-                first_product(t, lo, hi)
-            if t == 0:
-                for later, lo in ((2, 0), (3, 128)):
-                    pages.append(keep.tile([P, J], F32, name=f"page{later}", tag=f"d0_{lo}"))
-                    nc.gpsimd.memset(pages[later][:], 0.0)
+            first_product(t, EARLY if t < 2 else 0, I)
             nc.scalar.activation(out=slopes[t][:], in_=z_rows[:, t, :], func=RELU, scale=2.0)
             if t < 2:
-                nc.gpsimd.tensor_tensor(out=low_planes[:, t, :], in0=pages[t][:], in1=slopes[t][:], op=MULT)
-            if t == 1:
-                for q in range(quarters):
-                    cols = slice(q * QUARTER, (q + 1) * QUARTER)
-                    nc.scalar.copy(out=pairs[q][:, 0], in_=low_planes[:, :, cols].rearrange("p e j -> p j e"))
+                for h in range(J // BANK):
+                    cols = slice(h * BANK, (h + 1) * BANK)
+                    nc.gpsimd.tensor_tensor(out=low_planes[h][:, t, :], in0=pages[t][:, cols], in1=slopes[t][:, cols], op=MULT)
+                    if t == 1:
+                        for part in range(0, BANK, QUARTER):
+                            nc.scalar.copy(
+                                out=pairs[(h * BANK + part) // QUARTER][:, 0],
+                                in_=low_planes[h][:, :, part : part + QUARTER].rearrange("p e j -> p j e"),
+                            )
             if t == 2:
-                for q in range(quarters):
-                    cols = slice(q * QUARTER, (q + 1) * QUARTER)
-                    nc.gpsimd.tensor_tensor(out=third[q][:], in0=pages[t][:, cols], in1=slopes[t][:, cols], op=MULT)
-                    nc.scalar.copy(out=pairs[q][:, 1], in_=third[q][:].unsqueeze(2).to_broadcast([P, QUARTER, 2]))
+                for first, last in ((0, 2), (2, 3), (3, 4)):
+                    cols = slice(first * QUARTER, last * QUARTER)
+                    third = keep.tile([P, last - first, QUARTER], BF16, name=f"third{first}", tag=f"third{first}", align_bytes=64)
+                    nc.gpsimd.tensor_tensor(out=third[:].rearrange("p q j -> p (q j)"), in0=pages[t][:, cols], in1=slopes[t][:, cols], op=MULT)
+                    for q in range(first, last):
+                        nc.scalar.copy(out=pairs[q][:, 1], in_=third[:, q - first].unsqueeze(2).to_broadcast([P, QUARTER, 2]))
 
         wu_codes = keep.tile([P, K], I32, name="wu_codes", tag="then_wu", align_bytes=64)
         wu_plane = keep.tile([P, 1, K], U8, name="wu_plane", tag="then_wu_plane", align_bytes=64)
@@ -128,9 +134,10 @@ def tile_list_listed_slots_back_through_rest_kernel(
         sums = []
         for q in range(quarters):
             cols = slice(q * QUARTER, (q + 1) * QUARTER)
-            h, part = divmod(q * QUARTER, BANK)
             nc.vector.tensor_tensor(out=pairs[q][:, 1, :, 1], in0=pages[3][:, cols], in1=slopes[3][:, cols], op=MULT)
-            grouped = keep.tile([P, QUARTER * PACK], BF16, name=f"grouped{q}", align_bytes=64)
+        for q in range(quarters):
+            h, part = divmod(q * QUARTER, BANK)
+            grouped = keep.tile([P, QUARTER * PACK], BF16, name=f"grouped{q}", tag=f"third{3 if q == 0 else 4 + q}", align_bytes=64)
             nc.scalar.copy(
                 out=grouped[:].bitcast(F32).rearrange("p (j u) -> p j u", u=2),
                 in_=pairs[q][:].rearrange("p u j e -> p u (j e)").bitcast(F32).rearrange("p u j -> p j u"),
@@ -157,4 +164,5 @@ def tile_list_listed_slots_back_through_rest_kernel(
             cols = slice(h * BANK, (h + 1) * BANK)
             result = keep.tile([P, BANK], F32, name=f"result{h}_{m}")
             nc.vector.tensor_tensor(out=result[:], in0=acc[:], in1=run_rows[:, m, cols], op=ADD)
-            nc.sync.dma_start(out=out[m * P : (m + 1) * P, cols], in_=result[:])
+            queue = nc.scalar if m % 2 else nc.sync
+            queue.dma_start(out=out[m * P : (m + 1) * P, cols], in_=result[:])

@@ -21,15 +21,22 @@ P = 128
 PACK = 4
 PASSES = N // (P * PACK)
 BANK = 512
+HALVES = J // BANK
 QUARTER = 256
+QUARTERS = J // QUARTER
+LIST_GROUP = 16
+QUADRANT = 32
+SCALE_ROWS = 4
 EARLY = 128
+EARLY_PAGES = 2
+THIRD_RUNS = ((0, 2), (2, 3), (3, 4))
 
 
 def load_scale_rows(queues, plane, scales):
     for quad, queue in enumerate(queues):
         queue.dma_start(
-            out=plane[32 * quad : 32 * quad + 4].bitcast(I32),
-            in_=scales[:, 4 * quad : 4 * quad + 4, :].rearrange("z r c -> r z c").bitcast(I32),
+            out=plane[QUADRANT * quad : QUADRANT * quad + SCALE_ROWS].bitcast(I32),
+            in_=scales[:, SCALE_ROWS * quad : SCALE_ROWS * (quad + 1), :].rearrange("a s c -> s a c").bitcast(I32),
         )
 
 
@@ -41,8 +48,9 @@ def tile_list_listed_slots_back_through_rest_kernel(
         keep = ctx.enter_context(tc.tile_pool(name="keep", bufs=1))
         psum = ctx.enter_context(tc.psum_pool(name="psum", bufs=8))
 
-        offsets = keep.tile([P, I // 16], U16, name="offsets")
+        offsets = keep.tile([P, I // LIST_GROUP], U16, name="offsets")
         nc.sync.dma_start(offsets[:], offs)
+
         wd_raw = keep.tile([P, PASSES, 2 * R], U8, name="wd_raw", tag="then_z", align_bytes=64)
         wd_plane_raw = keep.tile([P, PASSES, R], U8, name="wd_plane_raw", tag="then_run", align_bytes=64)
         g_codes = keep.tile([P, PASSES, I], I32, name="g_codes", tag="then_wu", align_bytes=64)
@@ -50,20 +58,20 @@ def tile_list_listed_slots_back_through_rest_kernel(
 
         nc.gpsimd.memset(wd_plane_raw[:].bitcast(I32), 0)
         load_scale_rows((nc.sync, nc.sync, nc.scalar, nc.scalar), g_plane, g_scales)
-        nc.sync.dma_start(out=wd_raw[:].bitcast(I32), in_=wd_words.rearrange("z p c -> p z c").bitcast(I32))
-        g_rows = g_words.rearrange("z p c t -> p z (c t)").bitcast(I32)
+        nc.sync.dma_start(out=wd_raw[:].bitcast(I32), in_=wd_words.rearrange("a p c -> p a c").bitcast(I32))
+        g_rows = g_words.rearrange("a p c t -> p a (c t)").bitcast(I32)
         nc.sync.dma_start(out=g_codes[:, :, :EARLY], in_=g_rows[:, :, :EARLY])
-        load_scale_rows((nc.sync,) * 4, wd_plane_raw, wd_scales)
+        load_scale_rows((nc.sync,) * (P // QUADRANT), wd_plane_raw, wd_scales)
         nc.sync.dma_start(out=g_codes[:, :, EARLY:], in_=g_rows[:, :, EARLY:])
 
-        pages = [keep.tile([P, J], F32, name=f"page{t}") for t in range(2)]
-        for t in range(2):
+        pages = [keep.tile([P, J], F32, name=f"page{t}") for t in range(EARLY_PAGES)]
+        for t in range(EARLY_PAGES):
             nc.vector.memset(pages[t][:], 0.0)
 
         wd_codes = [keep.tile([P, PASSES, 2 * P], U8, name=f"wd_codes{t}", align_bytes=64) for t in range(PACK)]
         wd_planes = [keep.tile([P, PASSES, P], U8, name=f"wd_plane{t}", align_bytes=64) for t in range(PACK)]
-        wd_dealt = wd_raw[:].bitcast(U16).rearrange("p z (m t) -> p t z m", t=PACK)
-        plane_dealt = wd_plane_raw[:].rearrange("p z (m t) -> p t z m", t=PACK)
+        wd_dealt = wd_raw[:].bitcast(U16).rearrange("p a (m t) -> p t a m", t=PACK)
+        plane_dealt = wd_plane_raw[:].rearrange("p a (m t) -> p t a m", t=PACK)
         for t in range(PACK):
             nc.vector.tensor_copy(out=wd_codes[t][:].bitcast(U16), in_=wd_dealt[:, t])
             nc.vector.tensor_copy(out=wd_planes[t][:], in_=plane_dealt[:, t])
@@ -76,7 +84,7 @@ def tile_list_listed_slots_back_through_rest_kernel(
         for m in range(K // P):
             nc.sync.dma_start(out=run_rows[:, m, :], in_=run[m * P : (m + 1) * P, :])
 
-        def first_product(t, lo, hi):
+        def product_and_scatter(t, lo, hi):
             acc = psum.tile([P, BANK], F32, name="acc")
             step = BANK if hi - lo == BANK else P
             for c in range(lo, hi, step):
@@ -90,62 +98,78 @@ def tile_list_listed_slots_back_through_rest_kernel(
                         start=(a == 0),
                         stop=(a == PASSES - 1),
                     )
-            d = keep.tile([P, hi - lo], F32, name=f"d{t}_{lo}", tag=f"d{t}_{lo}" if hi == EARLY else f"rest{t}")
+            d = keep.tile([P, hi - lo], F32, name=f"d{t}_{lo}", tag=f"early{t}" if hi == EARLY else f"rest{t}")
             nc.scalar.copy(out=d[:], in_=acc[:, : hi - lo])
-            nc.vector.tensor_copy(pages[t][:].indirect(offsets[:, lo // 16 : hi // 16]), d[:])
+            nc.vector.tensor_copy(pages[t][:].indirect(offsets[:, lo // LIST_GROUP : hi // LIST_GROUP]), d[:])
 
-        quarters = J // QUARTER
         slopes = [keep.tile([P, J], F32, name=f"slope{t}") for t in range(PACK)]
-        low_planes = [keep.tile([P, 2, BANK], BF16, name=f"low_planes{h}") for h in range(J // BANK)]
-        pairs = [keep.tile([P, 2, QUARTER, 2], BF16, name=f"pairs{q}") for q in range(quarters)]
+        low_rows = [keep.tile([P, 2, BANK], BF16, name=f"low_rows{h}") for h in range(HALVES)]
+        pairs = [keep.tile([P, 2, QUARTER, 2], BF16, name=f"pairs{q}") for q in range(QUARTERS)]
 
-        for t in range(2):
-            first_product(t, 0, EARLY)
-            pages.append(keep.tile([P, J], F32, name=f"page{t + 2}", tag=f"d{t}_0"))
-            nc.gpsimd.memset(pages[t + 2][:], 0.0)
+        for t in range(EARLY_PAGES):
+            product_and_scatter(t, 0, EARLY)
+            later = EARLY_PAGES + t
+            pages.append(keep.tile([P, J], F32, name=f"page{later}", tag=f"early{t}"))
+            nc.gpsimd.memset(pages[later][:], 0.0)
+
+        def multiply_low(t):
+            for h in range(HALVES):
+                cols = slice(h * BANK, (h + 1) * BANK)
+                nc.gpsimd.tensor_tensor(out=low_rows[h][:, t, :], in0=pages[t][:, cols], in1=slopes[t][:, cols], op=MULT)
+                if t == 1:
+                    for part in range(0, BANK, QUARTER):
+                        nc.scalar.copy(
+                            out=pairs[(h * BANK + part) // QUARTER][:, 0],
+                            in_=low_rows[h][:, :, part : part + QUARTER].rearrange("p e j -> p j e"),
+                        )
+
+        def multiply_third():
+            for first, last in THIRD_RUNS:
+                cols = slice(first * QUARTER, last * QUARTER)
+                third = keep.tile(
+                    [P, last - first, QUARTER], BF16, name=f"third{first}", tag=f"third{first}", align_bytes=64
+                )
+                nc.gpsimd.tensor_tensor(
+                    out=third[:].rearrange("p q j -> p (q j)"), in0=pages[2][:, cols], in1=slopes[2][:, cols], op=MULT
+                )
+                for q in range(first, last):
+                    nc.scalar.copy(
+                        out=pairs[q][:, 1], in_=third[:, q - first].unsqueeze(2).to_broadcast([P, QUARTER, 2])
+                    )
+
         for t in range(PACK):
-            first_product(t, EARLY if t < 2 else 0, I)
+            product_and_scatter(t, EARLY if t < EARLY_PAGES else 0, I)
             nc.scalar.activation(out=slopes[t][:], in_=z_rows[:, t, :], func=RELU, scale=2.0)
             if t < 2:
-                for h in range(J // BANK):
-                    cols = slice(h * BANK, (h + 1) * BANK)
-                    nc.gpsimd.tensor_tensor(out=low_planes[h][:, t, :], in0=pages[t][:, cols], in1=slopes[t][:, cols], op=MULT)
-                    if t == 1:
-                        for part in range(0, BANK, QUARTER):
-                            nc.scalar.copy(
-                                out=pairs[(h * BANK + part) // QUARTER][:, 0],
-                                in_=low_planes[h][:, :, part : part + QUARTER].rearrange("p e j -> p j e"),
-                            )
+                multiply_low(t)
             if t == 2:
-                for first, last in ((0, 2), (2, 3), (3, 4)):
-                    cols = slice(first * QUARTER, last * QUARTER)
-                    third = keep.tile([P, last - first, QUARTER], BF16, name=f"third{first}", tag=f"third{first}", align_bytes=64)
-                    nc.gpsimd.tensor_tensor(out=third[:].rearrange("p q j -> p (q j)"), in0=pages[t][:, cols], in1=slopes[t][:, cols], op=MULT)
-                    for q in range(first, last):
-                        nc.scalar.copy(out=pairs[q][:, 1], in_=third[:, q - first].unsqueeze(2).to_broadcast([P, QUARTER, 2]))
+                multiply_third()
 
         wu_codes = keep.tile([P, K], I32, name="wu_codes", tag="then_wu", align_bytes=64)
         wu_plane = keep.tile([P, 1, K], U8, name="wu_plane", tag="then_wu_plane", align_bytes=64)
         nc.sync.dma_start(out=wu_codes[:], in_=wu_words[0].rearrange("p c t -> p (c t)").bitcast(I32))
-        load_scale_rows((nc.sync,) * 4, wu_plane, wu_scales)
+        load_scale_rows((nc.sync,) * (P // QUADRANT), wu_plane, wu_scales)
 
-        dz_codes = [keep.tile([P, BANK], I32, name=f"dz_codes{h}", align_bytes=64) for h in range(J // BANK)]
-        dz_planes = [keep.tile([P, BANK], U8, name=f"dz_plane{h}", align_bytes=64) for h in range(J // BANK)]
-        sums = []
-        for q in range(quarters):
+        dz_codes = [keep.tile([P, BANK], I32, name=f"dz_codes{h}", align_bytes=64) for h in range(HALVES)]
+        dz_planes = [keep.tile([P, BANK], U8, name=f"dz_plane{h}", align_bytes=64) for h in range(HALVES)]
+
+        for q in range(QUARTERS):
             cols = slice(q * QUARTER, (q + 1) * QUARTER)
             nc.vector.tensor_tensor(out=pairs[q][:, 1, :, 1], in0=pages[3][:, cols], in1=slopes[3][:, cols], op=MULT)
-        for q in range(quarters):
+
+        products = []
+        for q in range(QUARTERS):
             h, part = divmod(q * QUARTER, BANK)
-            grouped = keep.tile([P, QUARTER * PACK], BF16, name=f"grouped{q}", tag=f"third{3 if q == 0 else 4 + q}", align_bytes=64)
+            tag = f"third{THIRD_RUNS[-1][0]}" if q == 0 else f"woven{q}"
+            woven = keep.tile([P, QUARTER * PACK], BF16, name=f"woven{q}", tag=tag, align_bytes=64)
             nc.scalar.copy(
-                out=grouped[:].bitcast(F32).rearrange("p (j u) -> p j u", u=2),
+                out=woven[:].bitcast(F32).rearrange("p (j u) -> p j u", u=2),
                 in_=pairs[q][:].rearrange("p u j e -> p u (j e)").bitcast(F32).rearrange("p u j -> p j u"),
             )
             nc.vector.quantize_mx(
                 out=dz_codes[h][:, part : part + QUARTER].bitcast(E5M2),
                 scales=dz_planes[h][:, part : part + QUARTER],
-                in_=grouped[:],
+                in_=woven[:],
             )
             if part + QUARTER == BANK:
                 for m in range(K // P):
@@ -159,10 +183,17 @@ def tile_list_listed_slots_back_through_rest_kernel(
                         start=True,
                         stop=True,
                     )
-                    sums.append((h, m, acc))
-        for h, m, acc in sums:
+                    products.append((h, m, acc))
+
+        for h, m, acc in products:
             cols = slice(h * BANK, (h + 1) * BANK)
             result = keep.tile([P, BANK], F32, name=f"result{h}_{m}")
-            nc.vector.tensor_tensor(out=result[:], in0=acc[:], in1=run_rows[:, m, cols], op=ADD)
-            queue = nc.scalar if m % 2 else nc.sync
-            queue.dma_start(out=out[m * P : (m + 1) * P, cols], in_=result[:])
+            if (h, m) == (1, 0):
+                held = keep.tile([P, BANK], F32, name="held")
+                nc.scalar.copy(out=held[:], in_=acc[:])
+                nc.gpsimd.tensor_tensor(out=result[:], in0=held[:], in1=run_rows[:, m, cols], op=ADD)
+                nc.scalar.dma_start(out=out[m * P : (m + 1) * P, cols], in_=result[:])
+            else:
+                nc.vector.tensor_tensor(out=result[:], in0=acc[:], in1=run_rows[:, m, cols], op=ADD)
+                queue = nc.scalar if h == 0 and m % 2 else nc.sync
+                queue.dma_start(out=out[m * P : (m + 1) * P, cols], in_=result[:])

@@ -188,12 +188,12 @@ def tile_list_listed_slots_back_through_rest_kernel(
         for h, m, acc in products:
             cols = slice(h * BANK, (h + 1) * BANK)
             result = keep.tile([P, BANK], F32, name=f"result{h}_{m}")
-            if (h, m) == (1, 0):
+            if (h, m) == (0, 2):
                 held = keep.tile([P, BANK], F32, name="held")
                 nc.scalar.copy(out=held[:], in_=acc[:])
                 nc.gpsimd.tensor_tensor(out=result[:], in0=held[:], in1=run_rows[:, m, cols], op=ADD)
                 nc.scalar.dma_start(out=out[m * P : (m + 1) * P, cols], in_=result[:])
             else:
                 nc.vector.tensor_tensor(out=result[:], in0=acc[:], in1=run_rows[:, m, cols], op=ADD)
-                queue = nc.scalar if h == 0 and m % 2 else nc.sync
+                queue = nc.scalar if h == 1 and m == 2 else nc.sync
                 queue.dma_start(out=out[m * P : (m + 1) * P, cols], in_=result[:])

from contextlib import ExitStack

import concourse.mybir as mybir

N, R, K, J, I = 1024, 512, 512, 1024, 512
FLOPS = 2 * N * R * I + 2 * R * K * J

F32 = mybir.dt.float32
BF16 = mybir.dt.bfloat16
I32 = mybir.dt.int32
U16 = mybir.dt.uint16
U8 = mybir.dt.uint8
E4M3 = mybir.dt.float8_e4m3fn_x4
E5M2 = mybir.dt.float8_e5m2_x4
E2M1 = mybir.dt.float4_e2m1fn_x4
MULT = mybir.AluOpType.mult
ADD = mybir.AluOpType.add
RELU = mybir.ActivationFunctionType.Relu

P = 128
PACK = 4
PASSES = N // (P * PACK)
BANK = 512
HALVES = J // BANK
QUARTER = 256
QUARTERS = J // QUARTER
LIST_GROUP = 16
QUADRANT = 32
SCALE_ROWS = 4
EARLY = 128
EARLY_PAGES = 2
THIRD_RUNS = ((0, 2), (2, 3), (3, 4))


def load_scale_rows(queues, plane, scales):
    for quad, queue in enumerate(queues):
        queue.dma_start(
            out=plane[QUADRANT * quad : QUADRANT * quad + SCALE_ROWS].bitcast(I32),
            in_=scales[:, SCALE_ROWS * quad : SCALE_ROWS * (quad + 1), :].rearrange("a s c -> s a c").bitcast(I32),
        )


def tile_list_listed_slots_back_through_rest_kernel(
    tc, g_words, g_scales, wd_words, wd_scales, z, wu_words, wu_scales, run, offs, out
):
    nc = tc.nc
    with ExitStack() as ctx:
        keep = ctx.enter_context(tc.tile_pool(name="keep", bufs=1))
        psum = ctx.enter_context(tc.psum_pool(name="psum", bufs=8))

        offsets = keep.tile([P, I // LIST_GROUP], U16, name="offsets")
        nc.sync.dma_start(offsets[:], offs)

        wd_raw = keep.tile([P, PASSES, 2 * R], U8, name="wd_raw", tag="then_z", align_bytes=64)
        wd_plane_raw = keep.tile([P, PASSES, R], U8, name="wd_plane_raw", tag="then_run", align_bytes=64)
        g_codes = keep.tile([P, PASSES, I], I32, name="g_codes", tag="then_wu", align_bytes=64)
        g_plane = keep.tile([P, PASSES, I], U8, name="g_plane", tag="then_wu_plane", align_bytes=64)

        nc.gpsimd.memset(wd_plane_raw[:].bitcast(I32), 0)
        load_scale_rows((nc.sync, nc.sync, nc.scalar, nc.scalar), g_plane, g_scales)
        nc.sync.dma_start(out=wd_raw[:].bitcast(I32), in_=wd_words.rearrange("a p c -> p a c").bitcast(I32))
        g_rows = g_words.rearrange("a p c t -> p a (c t)").bitcast(I32)
        nc.sync.dma_start(out=g_codes[:, :, :EARLY], in_=g_rows[:, :, :EARLY])
        load_scale_rows((nc.sync,) * (P // QUADRANT), wd_plane_raw, wd_scales)
        nc.sync.dma_start(out=g_codes[:, :, EARLY:], in_=g_rows[:, :, EARLY:])

        pages = [keep.tile([P, J], F32, name=f"page{t}") for t in range(EARLY_PAGES)]
        for t in range(EARLY_PAGES):
            nc.vector.memset(pages[t][:], 0.0)

        wd_codes = [keep.tile([P, PASSES, 2 * P], U8, name=f"wd_codes{t}", align_bytes=64) for t in range(PACK)]
        wd_planes = [keep.tile([P, PASSES, P], U8, name=f"wd_plane{t}", align_bytes=64) for t in range(PACK)]
        wd_dealt = wd_raw[:].bitcast(U16).rearrange("p a (m t) -> p t a m", t=PACK)
        plane_dealt = wd_plane_raw[:].rearrange("p a (m t) -> p t a m", t=PACK)
        for t in range(PACK):
            nc.vector.tensor_copy(out=wd_codes[t][:].bitcast(U16), in_=wd_dealt[:, t])
            nc.vector.tensor_copy(out=wd_planes[t][:], in_=plane_dealt[:, t])

        z_rows = keep.tile([P, PACK, J], F32, name="z_rows", tag="then_z", align_bytes=64)
        z_dealt = z.rearrange("(p t) j -> p t j", t=PACK)
        for t in range(PACK):
            nc.sync.dma_start(out=z_rows[:, t, :], in_=z_dealt[:, t, :])
        run_rows = keep.tile([P, K // P, J], F32, name="run_rows", tag="then_run", align_bytes=64)
        for m in range(K // P):
            nc.sync.dma_start(out=run_rows[:, m, :], in_=run[m * P : (m + 1) * P, :])

        def product_and_scatter(t, lo, hi):
            acc = psum.tile([P, BANK], F32, name="acc")
            step = BANK if hi - lo == BANK else P
            for c in range(lo, hi, step):
                for a in range(PASSES):
                    nc.tensor.matmul_mx(
                        out=acc[:, c - lo : c - lo + step],
                        lhsT=wd_codes[t][:, a, :].bitcast(E2M1),
                        lhsT_scale=wd_planes[t][:, a, :],
                        rhs=g_codes[:, a, c : c + step].bitcast(E4M3),
                        rhs_scale=g_plane[:, a, c : c + step],
                        start=(a == 0),
                        stop=(a == PASSES - 1),
                    )
            d = keep.tile([P, hi - lo], F32, name=f"d{t}_{lo}", tag=f"early{t}" if hi == EARLY else f"rest{t}")
            nc.scalar.copy(out=d[:], in_=acc[:, : hi - lo])
            nc.vector.tensor_copy(pages[t][:].indirect(offsets[:, lo // LIST_GROUP : hi // LIST_GROUP]), d[:])

        slopes = [keep.tile([P, J], F32, name=f"slope{t}") for t in range(PACK)]
        low_rows = [keep.tile([P, 2, BANK], BF16, name=f"low_rows{h}") for h in range(HALVES)]
        pairs = [keep.tile([P, 2, QUARTER, 2], BF16, name=f"pairs{q}") for q in range(QUARTERS)]

        for t in range(EARLY_PAGES):
            product_and_scatter(t, 0, EARLY)
            later = EARLY_PAGES + t
            pages.append(keep.tile([P, J], F32, name=f"page{later}", tag=f"early{t}"))
            nc.gpsimd.memset(pages[later][:], 0.0)

        def multiply_low(t):
            for h in range(HALVES):
                cols = slice(h * BANK, (h + 1) * BANK)
                nc.gpsimd.tensor_tensor(out=low_rows[h][:, t, :], in0=pages[t][:, cols], in1=slopes[t][:, cols], op=MULT)
                if t == 1:
                    for part in range(0, BANK, QUARTER):
                        nc.scalar.copy(
                            out=pairs[(h * BANK + part) // QUARTER][:, 0],
                            in_=low_rows[h][:, :, part : part + QUARTER].rearrange("p e j -> p j e"),
                        )

        def multiply_third():
            for first, last in THIRD_RUNS:
                cols = slice(first * QUARTER, last * QUARTER)
                third = keep.tile(
                    [P, last - first, QUARTER], BF16, name=f"third{first}", tag=f"third{first}", align_bytes=64
                )
                nc.gpsimd.tensor_tensor(
                    out=third[:].rearrange("p q j -> p (q j)"), in0=pages[2][:, cols], in1=slopes[2][:, cols], op=MULT
                )
                for q in range(first, last):
                    nc.scalar.copy(
                        out=pairs[q][:, 1], in_=third[:, q - first].unsqueeze(2).to_broadcast([P, QUARTER, 2])
                    )

        for t in range(PACK):
            product_and_scatter(t, EARLY if t < EARLY_PAGES else 0, I)
            nc.scalar.activation(out=slopes[t][:], in_=z_rows[:, t, :], func=RELU, scale=2.0)
            if t < 2:
                multiply_low(t)
            if t == 2:
                multiply_third()

        wu_codes = keep.tile([P, K], I32, name="wu_codes", tag="then_wu", align_bytes=64)
        wu_plane = keep.tile([P, 1, K], U8, name="wu_plane", tag="then_wu_plane", align_bytes=64)
        nc.sync.dma_start(out=wu_codes[:], in_=wu_words[0].rearrange("p c t -> p (c t)").bitcast(I32))
        load_scale_rows((nc.sync,) * (P // QUADRANT), wu_plane, wu_scales)

        dz_codes = [keep.tile([P, BANK], I32, name=f"dz_codes{h}", align_bytes=64) for h in range(HALVES)]
        dz_planes = [keep.tile([P, BANK], U8, name=f"dz_plane{h}", align_bytes=64) for h in range(HALVES)]

        for q in range(QUARTERS):
            cols = slice(q * QUARTER, (q + 1) * QUARTER)
            nc.vector.tensor_tensor(out=pairs[q][:, 1, :, 1], in0=pages[3][:, cols], in1=slopes[3][:, cols], op=MULT)

        products = []
        for q in range(QUARTERS):
            h, part = divmod(q * QUARTER, BANK)
            tag = f"third{THIRD_RUNS[-1][0]}" if q == 0 else f"woven{q}"
            woven = keep.tile([P, QUARTER * PACK], BF16, name=f"woven{q}", tag=tag, align_bytes=64)
            nc.scalar.copy(
                out=woven[:].bitcast(F32).rearrange("p (j u) -> p j u", u=2),
                in_=pairs[q][:].rearrange("p u j e -> p u (j e)").bitcast(F32).rearrange("p u j -> p j u"),
            )
            nc.vector.quantize_mx(
                out=dz_codes[h][:, part : part + QUARTER].bitcast(E5M2),
                scales=dz_planes[h][:, part : part + QUARTER],
                in_=woven[:],
            )
            if part + QUARTER == BANK:
                for m in range(K // P):
                    acc = psum.tile([P, BANK], F32, name="acc")
                    nc.tensor.matmul_mx(
                        out=acc[:],
                        lhsT=wu_codes[:, m * P : (m + 1) * P].bitcast(E4M3),
                        lhsT_scale=wu_plane[:, 0, m * P : (m + 1) * P],
                        rhs=dz_codes[h][:].bitcast(E5M2),
                        rhs_scale=dz_planes[h][:],
                        start=True,
                        stop=True,
                    )
                    products.append((h, m, acc))

        for h, m, acc in products:
            cols = slice(h * BANK, (h + 1) * BANK)
            result = keep.tile([P, BANK], F32, name=f"result{h}_{m}")
            if (h, m) == (0, 2):
                held = keep.tile([P, BANK], F32, name="held")
                nc.scalar.copy(out=held[:], in_=acc[:])
                nc.gpsimd.tensor_tensor(out=result[:], in0=held[:], in1=run_rows[:, m, cols], op=ADD)
                nc.scalar.dma_start(out=out[m * P : (m + 1) * P, cols], in_=result[:])
            else:
                nc.vector.tensor_tensor(out=result[:], in0=acc[:], in1=run_rows[:, m, cols], op=ADD)
                queue = nc.scalar if h == 1 and m == 2 else nc.sync
                queue.dma_start(out=out[m * P : (m + 1) * P, cols], in_=result[:])
